import numpy as np
import ml_dtypes


def mxq(x, axis, fmt="e4m3"):
    dtype, down = {"e4m3": (ml_dtypes.float8_e4m3fn, 7), "e5m2": (ml_dtypes.float8_e5m2, 14)}[fmt]
    v = np.moveaxis(np.asarray(x, np.float32).astype(ml_dtypes.bfloat16).astype(np.float64), axis, -1)
    blocks = v.reshape(v.shape[:-1] + (-1, 32))
    amax = np.abs(blocks).max(-1, keepdims=True)
    byte = np.maximum(np.where(amax > 0, np.frexp(amax)[1] - 1 + 127, 0) - down, 1)
    scale = np.exp2(byte - 127.0)
    codes = (blocks / scale).astype(np.float32).astype(dtype).astype(np.float64)
    return np.moveaxis((codes * scale).reshape(v.shape), -1, axis)


WIDE = False


def mx_kscale(k):
    if not WIDE:
        return np.ones(k)
    levels = np.array([10, -10, 5, -5, 0])
    if k % 512:
        return np.exp2(np.random.permutation(np.resize(levels, k // 32))).repeat(32)
    a = np.empty((k // 512, 16))
    for p in range(k // 512):
        a[p, :8] = np.random.permutation(np.resize(levels, 8))
        for g in range(8):
            far = levels[np.abs(levels - a[p, g]) >= 10]
            a[p, g + 8] = far[np.random.randint(len(far))]
    return np.exp2(a.ravel()).repeat(32)


def f64(x):
    return np.asarray(x).astype(np.float64)


def striped(idx):
    return np.tile(idx.reshape(-1, 16).T, (8, 1)).astype(np.uint16)


def unstriped(offs):
    return offs[:16].T.reshape(-1).astype(np.int64)


def pack_weight(w):
    k, n = w.shape
    w = f64(np.asarray(w, np.float32).astype(ml_dtypes.bfloat16)).reshape(k // 32, 32, n)
    amax = np.abs(w).max(1)
    byte = np.clip(np.where(amax > 0, np.frexp(amax)[1] - 1 + 127 - 7, 1), 1, 254)
    scaled = (w * np.exp2(127.0 - byte)[:, None, :]).reshape(k, n).astype(np.float32)
    words = np.ascontiguousarray(scaled.reshape(k // 512, 128, 4, n).transpose(0, 1, 3, 2)).astype(ml_dtypes.float8_e4m3fn).view(np.uint8)
    return words, np.ascontiguousarray(byte.astype(np.uint8).reshape(k // 512, 16, n))


def unpack_weight(words, scales):
    g, p, n, _ = words.shape
    vals = np.ascontiguousarray(words).view(ml_dtypes.float8_e4m3fn).astype(np.float64) * np.repeat(np.exp2(scales.astype(np.float64) - 127.0), 8, axis=1)[..., None]
    return vals.transpose(0, 1, 3, 2).reshape(g * 512, n)


def relu(v):
    return np.maximum(v, 0.0)


K, T, S, H, Z, A = 512, 2048, 512, 512, 128, 512


def setup_inputs():
    n = np.random.standard_normal
    s = mx_kscale(K)[:, None]
    u = mx_kscale(H)
    packed_xT = pack_weight(n((K, T)) * s)
    return {
        "x_words": packed_xT[0],
        "x_scales": packed_xT[1],
        "w1": (n((K, H)) / np.sqrt(K) / s * u).astype(np.float32),
        "wv": (n((H, Z)) / np.sqrt(H) / u[:, None]).astype(np.float32),
        "wa": (n((H, A)) / np.sqrt(H) / u[:, None]).astype(np.float32),
        "isw": (np.random.uniform(0.3, 1.5, (S, 1))).astype(np.float32),
        "offs": striped(np.random.permutation(T)[:S]),
    }


def reference(x_words, x_scales, w1, wv, wa, isw, offs):
    xq = unpack_weight(x_words, x_scales)[:, unstriped(offs)]
    h = relu(mxq(f64(w1), 0, "e4m3").T @ xq)
    hq = mxq(h, 0, "e4m3")
    wvq = mxq(f64(wv), 0, "e4m3")
    vv = hq.T @ wvq
    waq = mxq(f64(wa), 0, "e4m3")
    a = hq.T @ waq
    a0 = a[:, :Z]
    a1 = a[:, Z:2 * Z]
    a2 = a[:, 2 * Z:3 * Z]
    a3 = a[:, 3 * Z:4 * Z]
    mean = 0.25 * (a0 + a1 + a2 + a3)
    y = vv + np.maximum(np.maximum(np.maximum(a0, a1), a2), a3) - mean
    ex = np.exp(y - y.max(axis=1, keepdims=True))
    return f64(isw) * (ex / ex.sum(axis=1, keepdims=True))

@@ -1,0 +1,191 @@
+from contextlib import ExitStack
+
+import concourse.mybir as mybir
+from concourse.masks import make_identity
+
+F32 = mybir.dt.float32
+BF16 = mybir.dt.bfloat16
+I32 = mybir.dt.int32
+U32 = mybir.dt.uint32
+U16 = mybir.dt.uint16
+U8 = mybir.dt.uint8
+X4 = mybir.dt.float8_e4m3fn_x4
+ALU = mybir.AluOpType
+ACT = mybir.ActivationFunctionType
+AX = mybir.AxisListType
+
+P = 128
+K, T, S, H, Z, A = 512, 2048, 512, 512, 128, 512
+FLOPS = 2 * S * (K * H + H * Z + H * A)
+
+
+def tile_picked_yduel_dist_p_kernel(tc, x_words, x_scales, w1, wv, wa, isw, offs, out):
+    nc = tc.nc
+    with ExitStack() as ctx:
+        keep = ctx.enter_context(tc.tile_pool(name="keep", bufs=1))
+        late = ctx.enter_context(tc.tile_pool(name="late", bufs=1))
+        psum = ctx.enter_context(tc.psum_pool(name="psum", bufs=1))
+
+        def sb(name, shape, dtype):
+            return keep.tile(shape, dtype, name=name, align_bytes=64)
+
+        def quantize(codes, scales, values):
+            nc.vector.quantize_mx(out=codes.bitcast(X4), scales=scales, in_=values)
+
+        def product(dst, lhs, rhs, start=True, stop=True):
+            nc.tensor.matmul_mx(dst, lhsT=lhs[0].bitcast(X4), lhsT_scale=lhs[1], rhs=rhs[0].bitcast(X4), rhs_scale=rhs[1], start=start, stop=stop)
+
+        offsets = keep.tile([P, S // 16], U16, name="offsets")
+        nc.sync.dma_start(offsets[:], offs)
+        w1_rows = w1.rearrange("(p j) c -> p j c", j=4)
+        wa_rows = wa.rearrange("(p j) c -> p j c", j=4)
+        w1_raw = [sb(f"w1_raw{u}", [P, 4, 256], F32) for u in range(2)]
+        for u in range(2):
+            nc.sync.dma_start(w1_raw[u][:], w1_rows[:, :, 256 * u : 256 * (u + 1)])
+
+        xs_all = sb("xs_all", [P, T], U8)
+        nc.vector.memset(xs_all[:].bitcast(I32), 0)
+        for q in range(4):
+            nc.sync.dma_start(xs_all[32 * q : 32 * q + 4, :].bitcast(I32), x_scales[0][4 * q : 4 * q + 4, :].bitcast(I32))
+        warm = late.tile([P, 4616], F32, name="warm", offset=0)
+        nc.vector.memset(warm[:, 0:1], 0.0)
+        nc.scalar.activation(warm[:, 8:9], warm[:, 0:1], ACT.Exp)
+
+        xw_all = late.tile([P, T], U32, name="xw_all", offset=0)
+        nc.sync.dma_start(xw_all[:].bitcast(I32), x_words[0].rearrange("p n t -> p (n t)").bitcast(I32))
+        wa_raw = [late.tile([P, 4, 256], F32, name=f"wa_raw{u}", offset=10240 + 4096 * u) for u in range(2)]
+        for u in (1, 0):
+            nc.sync.dma_start(wa_raw[u][:], wa_rows[:, :, 256 * u : 256 * (u + 1)])
+        wv_raw = late.tile([P, 4, Z], F32, name="wv_raw", offset=8192)
+        nc.sync.dma_start(wv_raw[:], wv.rearrange("(p j) c -> p j c", j=4))
+        isw_sb = late.tile([P, 4], F32, name="isw_sb", offset=18432)
+        with nc.allow_non_contiguous_dma(reason="one weight a partition"):
+            nc.sync.dma_start(isw_sb[:], isw.rearrange("(c p) o -> p (c o)", p=P))
+        ident = sb("ident", [P, P], F32)
+        make_identity(nc, ident[:])
+
+        w1_codes = sb("w1_codes", [P, H], U32)
+        w1_scales = sb("w1_scales", [P, H], U8)
+        w1_bf = sb("w1_bf", [P, 4, P, 4], BF16)
+        for u in range(2):
+            dst = w1_bf[:, :, 64 * u : 64 * (u + 1), :].rearrange("p t m j -> p m t j")
+            src = w1_raw[u][:].rearrange("p j (m t) -> p m t j", t=4)
+            nc.vector.tensor_copy(dst, src)
+        quantize(w1_codes[:], w1_scales[:], w1_bf[:].rearrange("p t m j -> p (t m j)"))
+
+        xs = sb("xs", [P, S], U8)
+        nc.vector.tensor_copy(xs[:], xs_all[:].indirect(offsets[:]))
+        xw = [sb(f"xw{u}", [P, 256], U32) for u in range(2)]
+        for u in range(2):
+            nc.vector.tensor_copy(xw[u][:], xw_all[:].indirect(offsets[:, 16 * u : 16 * (u + 1)]))
+
+        wa_bf = [sb(f"wa_bf{u}", [P, 256, 4], BF16) for u in range(2)]
+        nc.scalar.copy(wa_bf[1][:, Z:], wa_raw[1][:, :, Z:].rearrange("p j c -> p c j"))
+        nc.vector.tensor_copy(wa_bf[1][:, :Z], wa_raw[1][:, :, :Z].rearrange("p j c -> p c j"))
+
+        h_bf = []
+        for b in range(4):
+            bank = psum.tile([P, 4, P], F32, name=f"h_bank{b % 2}")
+            for t in range(4):
+                product(bank[:, t, :], (w1_codes[:, P * t : P * (t + 1)], w1_scales[:, P * t : P * (t + 1)]), (xw[b // 2][:, P * (b % 2) : P * (b % 2 + 1)], xs[:, P * b : P * (b + 1)]))
+            h_bf.append(sb(f"h_bf{b}", [P, P, 4], BF16))
+            nc.scalar.activation(h_bf[b][:], bank[:].rearrange("p t n -> p n t"), ACT.Relu)
+        h_q = [(sb(f"h_codes{u}", [P, 256], U32), sb(f"h_scales{u}", [P, 256], U8)) for u in range(2)]
+
+        wa_q = [(sb(f"wa_codes{u}", [P, 256], U32), sb(f"wa_scales{u}", [P, 256], U8)) for u in range(2)]
+        wv_q = (sb("wv_codes", [P, Z], U32), sb("wv_scales", [P, Z], U8))
+        wv_bf = sb("wv_bf", [P, Z, 4], BF16)
+
+        def quantize_wa(u):
+            quantize(wa_q[u][0][:], wa_q[u][1][:], wa_bf[u][:].rearrange("p c j -> p (c j)"))
+
+        def quantize_h(b):
+            cols = slice(P * (b % 2), P * (b % 2 + 1))
+            quantize(h_q[b // 2][0][:, cols], h_q[b // 2][1][:, cols], h_bf[b][:].rearrange("p n t -> p (n t)"))
+
+        quantize_wa(1)
+        nc.vector.tensor_copy(wa_bf[0][:], wa_raw[0][:].rearrange("p j c -> p c j"))
+        quantize_h(0)
+        quantize_wa(0)
+        quantize_h(1)
+        nc.vector.tensor_scalar(wv_bf[:], wv_raw[:].rearrange("p j c -> p c j"), -4.0, None, ALU.mult)
+        quantize_h(2)
+        quantize(wv_q[0][:], wv_q[1][:], wv_bf[:].rearrange("p c j -> p (c j)"))
+        quantize_h(3)
+
+        def action(a):
+            cols = slice(Z * (a % 2), Z * (a % 2 + 1))
+            return wa_q[a // 2][0][:, cols], wa_q[a // 2][1][:, cols]
+
+        value = (wv_q[0][:], wv_q[1][:])
+
+        def softmax(b, y):
+            neg_max = sb(f"neg_max{b}", [P, 1], F32)
+            nc.vector.tensor_reduce(neg_max[:], y, AX.X, ALU.max, negate=True)
+            ex = sb(f"ex{b}", [P, Z], F32)
+            total = sb(f"total{b}", [P, 1], F32)
+            nc.scalar.activation(ex[:], y, ACT.Exp, bias=neg_max[:], accum_out=total[:])
+            inv = sb(f"inv{b}", [P, 1], F32)
+            nc.vector.reciprocal(inv[:], total[:])
+            res = sb(f"res{b}", [P, Z], F32)
+            nc.vector.tensor_scalar(res[:], ex[:], inv[:], isw_sb[:, b : b + 1], ALU.mult, ALU.mult)
+            nc.sync.dma_start(out[P * b : P * (b + 1), :], res[:])
+
+        hi = psum.tile([P, 2, 256], F32, name="hi")
+        lo = psum.tile([P, 2, 256], F32, name="lo")
+        vv = psum.tile([P, 256], F32, name="vv")
+        h01 = (h_q[0][0][:], h_q[0][1][:])
+        for a in range(2):
+            product(hi[:, a], action(2 + a), h01)
+        for a in range(2):
+            product(lo[:, a], action(a), h01)
+        product(vv[:], value, h01)
+
+        def rows_products(b, g_name):
+            cols = slice(P * (b % 2), P * (b % 2 + 1))
+            h = (h_q[1][0][:, cols], h_q[1][1][:, cols])
+            adv = psum.tile([P, 4, Z], F32, name=f"adv{b}")
+            for u in range(2):
+                product(adv[:, 2 * u : 2 * u + 2].rearrange("p a z -> p (a z)"), h, (wa_q[u][0][:], wa_q[u][1][:]))
+            g = psum.tile([P, Z], F32, name=g_name)
+            for a in range(4):
+                product(g[:], h, action(a), a == 0, False)
+            product(g[:], h, value, False, True)
+            return adv, g
+
+        def rows_max(b, adv):
+            mx = sb(f"mx{b}", [P, Z], F32)
+            nc.vector.tensor_reduce(mx[:], adv[:].rearrange("p a z -> p z a"), AX.X, ALU.max)
+            return mx
+
+        def rows_logits(b, mx, g):
+            y = sb(f"y{b}", [P, Z], F32)
+            nc.vector.scalar_tensor_tensor(y[:], g[:], -0.25, mx[:], ALU.mult, ALU.add)
+            return y
+
+        adv2, g2 = rows_products(2, "g2")
+        adv3, g3 = rows_products(3, "h_bank1")
+
+        c23 = sb("c23", [P, 2, 256], F32)
+        nc.scalar.activation(c23[:], hi[:], ACT.Copy, scale=-0.25)
+        pair = sb("pair", [P, 2, 256], F32)
+        nc.vector.scalar_tensor_tensor(pair[:], c23[:], -4.0, lo[:], ALU.mult, ALU.max)
+        cv = sb("cv", [P, 256], F32)
+        nc.scalar.activation(cv[:], vv[:], ACT.Copy, scale=-0.25)
+        c01 = sb("c01", [P, 2, 256], F32)
+        nc.scalar.activation(c01[:], lo[:], ACT.Copy, scale=-0.25)
+        mx2 = rows_max(2, adv2)
+        best = sb("best", [P, 256], F32)
+        nc.vector.tensor_tensor(best[:], pair[:, 0], pair[:, 1], ALU.max)
+        mx3 = rows_max(3, adv3)
+        ys = [psum.tile([P, Z], F32, name=name) for name in ("h_bank0", "vv")]
+        terms = [c23[:, 0], c23[:, 1], cv[:], c01[:, 0], c01[:, 1], best[:]]
+        for n, term in enumerate(terms):
+            for i in range(2):
+                nc.tensor.matmul(ys[i][:], lhsT=term[:, P * i : P * (i + 1)], rhs=ident[:], is_transpose=True, start=n == 0, stop=n == len(terms) - 1)
+        y2 = rows_logits(2, mx2, g2)
+        y3 = rows_logits(3, mx3, g3)
+        softmax(2, y2[:])
+        softmax(0, ys[0][:])
+        softmax(1, ys[1][:])
+        softmax(3, y3[:])

@@ -46,7 +46,7 @@ def tile_picked_yduel_dist_p_kernel(tc, x_words, x_scales, w1, wv, wa, isw, offs
         xs_all = sb("xs_all", [P, T], U8)
         nc.vector.memset(xs_all[:].bitcast(I32), 0)
         for q in range(4):
-            nc.sync.dma_start(xs_all[32 * q : 32 * q + 4, :].bitcast(I32), x_scales[0][4 * q : 4 * q + 4, :].bitcast(I32))
+            nc.sync.dma_start(xs_all[q:P:32, :].bitcast(I32), x_scales[0][q:16:4, :].bitcast(I32))
         warm = late.tile([P, 4616], F32, name="warm", offset=0)
         nc.vector.memset(warm[:, 0:1], 0.0)
         nc.scalar.activation(warm[:, 8:9], warm[:, 0:1], ACT.Exp)
@@ -70,7 +70,11 @@ def tile_picked_yduel_dist_p_kernel(tc, x_words, x_scales, w1, wv, wa, isw, offs
         for u in range(2):
             dst = w1_bf[:, :, 64 * u : 64 * (u + 1), :].rearrange("p t m j -> p m t j")
             src = w1_raw[u][:].rearrange("p j (m t) -> p m t j", t=4)
-            nc.vector.tensor_copy(dst, src)
+            if u == 0:
+                nc.scalar.copy(dst, src)
+            else:
+                nc.scalar.copy(dst[:, 32:], src[:, 32:])
+                nc.vector.tensor_copy(dst[:, :32], src[:, :32])
         quantize(w1_codes[:], w1_scales[:], w1_bf[:].rearrange("p t m j -> p (t m j)"))
 
         xs = sb("xs", [P, S], U8)
@@ -85,10 +89,10 @@ def tile_picked_yduel_dist_p_kernel(tc, x_words, x_scales, w1, wv, wa, isw, offs
 
         h_bf = []
         for b in range(4):
-            bank = psum.tile([P, 4, P], F32, name=f"h_bank{b % 2}")
+            bank = psum.tile([P, 4, P], F32, name=f"h_bank{b}")
             for t in range(4):
                 product(bank[:, t, :], (w1_codes[:, P * t : P * (t + 1)], w1_scales[:, P * t : P * (t + 1)]), (xw[b // 2][:, P * (b % 2) : P * (b % 2 + 1)], xs[:, P * b : P * (b + 1)]))
-            h_bf.append(sb(f"h_bf{b}", [P, P, 4], BF16))
+            h_bf.append(late.tile([P, P, 4], BF16, name=f"h_bf{b}", offset=14336 + 1024 * b, align_bytes=64))
             nc.scalar.activation(h_bf[b][:], bank[:].rearrange("p t n -> p n t"), ACT.Relu)
         h_q = [(sb(f"h_codes{u}", [P, 256], U32), sb(f"h_scales{u}", [P, 256], U8)) for u in range(2)]
 
@@ -104,14 +108,15 @@ def tile_picked_yduel_dist_p_kernel(tc, x_words, x_scales, w1, wv, wa, isw, offs
             quantize(h_q[b // 2][0][:, cols], h_q[b // 2][1][:, cols], h_bf[b][:].rearrange("p n t -> p (n t)"))
 
         quantize_wa(1)
-        nc.vector.tensor_copy(wa_bf[0][:], wa_raw[0][:].rearrange("p j c -> p c j"))
         quantize_h(0)
-        quantize_wa(0)
         quantize_h(1)
-        nc.vector.tensor_scalar(wv_bf[:], wv_raw[:].rearrange("p j c -> p c j"), -4.0, None, ALU.mult)
+        for a in range(2):
+            nc.vector.tensor_copy(wa_bf[0][:, Z * a : Z * (a + 1)], wa_raw[0][:, :, Z * a : Z * (a + 1)].rearrange("p j c -> p c j"))
+        quantize_wa(0)
         quantize_h(2)
-        quantize(wv_q[0][:], wv_q[1][:], wv_bf[:].rearrange("p c j -> p (c j)"))
         quantize_h(3)
+        nc.vector.tensor_scalar(wv_bf[:], wv_raw[:].rearrange("p j c -> p c j"), -4.0, None, ALU.mult)
+        quantize(wv_q[0][:], wv_q[1][:], wv_bf[:].rearrange("p c j -> p (c j)"))
 
         def action(a):
             cols = slice(Z * (a % 2), Z * (a % 2 + 1))
@@ -141,10 +146,10 @@ def tile_picked_yduel_dist_p_kernel(tc, x_words, x_scales, w1, wv, wa, isw, offs
             product(lo[:, a], action(a), h01)
         product(vv[:], value, h01)
 
-        def rows_products(b, g_name):
+        def rows_products(b, adv_name, g_name):
             cols = slice(P * (b % 2), P * (b % 2 + 1))
             h = (h_q[1][0][:, cols], h_q[1][1][:, cols])
-            adv = psum.tile([P, 4, Z], F32, name=f"adv{b}")
+            adv = psum.tile([P, 4, Z], F32, name=adv_name)
             for u in range(2):
                 product(adv[:, 2 * u : 2 * u + 2].rearrange("p a z -> p (a z)"), h, (wa_q[u][0][:], wa_q[u][1][:]))
             g = psum.tile([P, Z], F32, name=g_name)
@@ -163,27 +168,27 @@ def tile_picked_yduel_dist_p_kernel(tc, x_words, x_scales, w1, wv, wa, isw, offs
             nc.vector.scalar_tensor_tensor(y[:], g[:], -0.25, mx[:], ALU.mult, ALU.add)
             return y
 
-        adv2, g2 = rows_products(2, "g2")
-        adv3, g3 = rows_products(3, "h_bank1")
+        adv2, g2 = rows_products(2, "adv2", "h_bank1")
+        adv3, g3 = rows_products(3, "h_bank0", "h_bank2")
 
         c23 = sb("c23", [P, 2, 256], F32)
         nc.scalar.activation(c23[:], hi[:], ACT.Copy, scale=-0.25)
+        c01 = sb("c01", [P, 2, 256], F32)
+        nc.scalar.activation(c01[:], lo[:], ACT.Copy, scale=-0.25)
         pair = sb("pair", [P, 2, 256], F32)
         nc.vector.scalar_tensor_tensor(pair[:], c23[:], -4.0, lo[:], ALU.mult, ALU.max)
         cv = sb("cv", [P, 256], F32)
         nc.scalar.activation(cv[:], vv[:], ACT.Copy, scale=-0.25)
-        c01 = sb("c01", [P, 2, 256], F32)
-        nc.scalar.activation(c01[:], lo[:], ACT.Copy, scale=-0.25)
-        mx2 = rows_max(2, adv2)
         best = sb("best", [P, 256], F32)
         nc.vector.tensor_tensor(best[:], pair[:, 0], pair[:, 1], ALU.max)
+        mx2 = rows_max(2, adv2)
+        y2 = rows_logits(2, mx2, g2)
         mx3 = rows_max(3, adv3)
-        ys = [psum.tile([P, Z], F32, name=name) for name in ("h_bank0", "vv")]
-        terms = [c23[:, 0], c23[:, 1], cv[:], c01[:, 0], c01[:, 1], best[:]]
+        ys = [psum.tile([P, Z], F32, name=name) for name in ("h_bank3", "hi")]
+        terms = [c23[:, 0], c23[:, 1], c01[:, 0], c01[:, 1], cv[:], best[:]]
         for n, term in enumerate(terms):
             for i in range(2):
                 nc.tensor.matmul(ys[i][:], lhsT=term[:, P * i : P * (i + 1)], rhs=ident[:], is_transpose=True, start=n == 0, stop=n == len(terms) - 1)
-        y2 = rows_logits(2, mx2, g2)
         y3 = rows_logits(3, mx3, g3)
         softmax(2, y2[:])
         softmax(0, ys[0][:])

from contextlib import ExitStack

import concourse.mybir as mybir
from concourse.masks import make_identity

F32 = mybir.dt.float32
BF16 = mybir.dt.bfloat16
I32 = mybir.dt.int32
U32 = mybir.dt.uint32
U16 = mybir.dt.uint16
U8 = mybir.dt.uint8
X4 = mybir.dt.float8_e4m3fn_x4
ALU = mybir.AluOpType
ACT = mybir.ActivationFunctionType
AX = mybir.AxisListType

P = 128
K, T, S, H, Z, A = 512, 2048, 512, 512, 128, 512
FLOPS = 2 * S * (K * H + H * Z + H * A)


def tile_picked_yduel_dist_p_kernel(tc, x_words, x_scales, w1, wv, wa, isw, offs, out):
    nc = tc.nc
    with ExitStack() as ctx:
        keep = ctx.enter_context(tc.tile_pool(name="keep", bufs=1))
        late = ctx.enter_context(tc.tile_pool(name="late", bufs=1))
        psum = ctx.enter_context(tc.psum_pool(name="psum", bufs=1))

        def sb(name, shape, dtype):
            return keep.tile(shape, dtype, name=name, align_bytes=64)

        def quantize(codes, scales, values):
            nc.vector.quantize_mx(out=codes.bitcast(X4), scales=scales, in_=values)

        def product(dst, lhs, rhs, start=True, stop=True):
            nc.tensor.matmul_mx(dst, lhsT=lhs[0].bitcast(X4), lhsT_scale=lhs[1], rhs=rhs[0].bitcast(X4), rhs_scale=rhs[1], start=start, stop=stop)

        offsets = keep.tile([P, S // 16], U16, name="offsets")
        nc.sync.dma_start(offsets[:], offs)
        w1_rows = w1.rearrange("(p j) c -> p j c", j=4)
        wa_rows = wa.rearrange("(p j) c -> p j c", j=4)
        w1_raw = [sb(f"w1_raw{u}", [P, 4, 256], F32) for u in range(2)]
        for u in range(2):
            nc.sync.dma_start(w1_raw[u][:], w1_rows[:, :, 256 * u : 256 * (u + 1)])

        xs_all = sb("xs_all", [P, T], U8)
        nc.vector.memset(xs_all[:].bitcast(I32), 0)
        for q in range(4):
            nc.sync.dma_start(xs_all[q:P:32, :].bitcast(I32), x_scales[0][q:16:4, :].bitcast(I32))
        warm = late.tile([P, 4616], F32, name="warm", offset=0)
        nc.vector.memset(warm[:, 0:1], 0.0)
        nc.scalar.activation(warm[:, 8:9], warm[:, 0:1], ACT.Exp)

        xw_all = late.tile([P, T], U32, name="xw_all", offset=0)
        nc.sync.dma_start(xw_all[:].bitcast(I32), x_words[0].rearrange("p n t -> p (n t)").bitcast(I32))
        wa_raw = [late.tile([P, 4, 256], F32, name=f"wa_raw{u}", offset=10240 + 4096 * u) for u in range(2)]
        for u in (1, 0):
            nc.sync.dma_start(wa_raw[u][:], wa_rows[:, :, 256 * u : 256 * (u + 1)])
        wv_raw = late.tile([P, 4, Z], F32, name="wv_raw", offset=8192)
        nc.sync.dma_start(wv_raw[:], wv.rearrange("(p j) c -> p j c", j=4))
        isw_sb = late.tile([P, 4], F32, name="isw_sb", offset=18432)
        with nc.allow_non_contiguous_dma(reason="one weight a partition"):
            nc.sync.dma_start(isw_sb[:], isw.rearrange("(c p) o -> p (c o)", p=P))
        ident = sb("ident", [P, P], F32)
        make_identity(nc, ident[:])

        w1_codes = sb("w1_codes", [P, H], U32)
        w1_scales = sb("w1_scales", [P, H], U8)
        w1_bf = sb("w1_bf", [P, 4, P, 4], BF16)
        for u in range(2):
            dst = w1_bf[:, :, 64 * u : 64 * (u + 1), :].rearrange("p t m j -> p m t j")
            src = w1_raw[u][:].rearrange("p j (m t) -> p m t j", t=4)
            if u == 0:
                nc.scalar.copy(dst, src)
            else:
                nc.scalar.copy(dst[:, 32:], src[:, 32:])
                nc.vector.tensor_copy(dst[:, :32], src[:, :32])
        quantize(w1_codes[:], w1_scales[:], w1_bf[:].rearrange("p t m j -> p (t m j)"))

        xs = sb("xs", [P, S], U8)
        nc.vector.tensor_copy(xs[:], xs_all[:].indirect(offsets[:]))
        xw = [sb(f"xw{u}", [P, 256], U32) for u in range(2)]
        for u in range(2):
            nc.vector.tensor_copy(xw[u][:], xw_all[:].indirect(offsets[:, 16 * u : 16 * (u + 1)]))

        wa_bf = [sb(f"wa_bf{u}", [P, 256, 4], BF16) for u in range(2)]
        nc.scalar.copy(wa_bf[1][:, Z:], wa_raw[1][:, :, Z:].rearrange("p j c -> p c j"))
        nc.vector.tensor_copy(wa_bf[1][:, :Z], wa_raw[1][:, :, :Z].rearrange("p j c -> p c j"))

        h_bf = []
        for b in range(4):
            bank = psum.tile([P, 4, P], F32, name=f"h_bank{b}")
            for t in range(4):
                product(bank[:, t, :], (w1_codes[:, P * t : P * (t + 1)], w1_scales[:, P * t : P * (t + 1)]), (xw[b // 2][:, P * (b % 2) : P * (b % 2 + 1)], xs[:, P * b : P * (b + 1)]))
            h_bf.append(late.tile([P, P, 4], BF16, name=f"h_bf{b}", offset=14336 + 1024 * b, align_bytes=64))
            nc.scalar.activation(h_bf[b][:], bank[:].rearrange("p t n -> p n t"), ACT.Relu)
        h_q = [(sb(f"h_codes{u}", [P, 256], U32), sb(f"h_scales{u}", [P, 256], U8)) for u in range(2)]

        wa_q = [(sb(f"wa_codes{u}", [P, 256], U32), sb(f"wa_scales{u}", [P, 256], U8)) for u in range(2)]
        wv_q = (sb("wv_codes", [P, Z], U32), sb("wv_scales", [P, Z], U8))
        wv_bf = sb("wv_bf", [P, Z, 4], BF16)

        def quantize_wa(u):
            quantize(wa_q[u][0][:], wa_q[u][1][:], wa_bf[u][:].rearrange("p c j -> p (c j)"))

        def quantize_h(b):
            cols = slice(P * (b % 2), P * (b % 2 + 1))
            quantize(h_q[b // 2][0][:, cols], h_q[b // 2][1][:, cols], h_bf[b][:].rearrange("p n t -> p (n t)"))

        quantize_wa(1)
        quantize_h(0)
        quantize_h(1)
        for a in range(2):
            nc.vector.tensor_copy(wa_bf[0][:, Z * a : Z * (a + 1)], wa_raw[0][:, :, Z * a : Z * (a + 1)].rearrange("p j c -> p c j"))
        quantize_wa(0)
        quantize_h(2)
        quantize_h(3)
        nc.vector.tensor_scalar(wv_bf[:], wv_raw[:].rearrange("p j c -> p c j"), -4.0, None, ALU.mult)
        quantize(wv_q[0][:], wv_q[1][:], wv_bf[:].rearrange("p c j -> p (c j)"))

        def action(a):
            cols = slice(Z * (a % 2), Z * (a % 2 + 1))
            return wa_q[a // 2][0][:, cols], wa_q[a // 2][1][:, cols]

        value = (wv_q[0][:], wv_q[1][:])

        def softmax(b, y):
            neg_max = sb(f"neg_max{b}", [P, 1], F32)
            nc.vector.tensor_reduce(neg_max[:], y, AX.X, ALU.max, negate=True)
            ex = sb(f"ex{b}", [P, Z], F32)
            total = sb(f"total{b}", [P, 1], F32)
            nc.scalar.activation(ex[:], y, ACT.Exp, bias=neg_max[:], accum_out=total[:])
            inv = sb(f"inv{b}", [P, 1], F32)
            nc.vector.reciprocal(inv[:], total[:])
            res = sb(f"res{b}", [P, Z], F32)
            nc.vector.tensor_scalar(res[:], ex[:], inv[:], isw_sb[:, b : b + 1], ALU.mult, ALU.mult)
            nc.sync.dma_start(out[P * b : P * (b + 1), :], res[:])

        hi = psum.tile([P, 2, 256], F32, name="hi")
        lo = psum.tile([P, 2, 256], F32, name="lo")
        vv = psum.tile([P, 256], F32, name="vv")
        h01 = (h_q[0][0][:], h_q[0][1][:])
        for a in range(2):
            product(hi[:, a], action(2 + a), h01)
        for a in range(2):
            product(lo[:, a], action(a), h01)
        product(vv[:], value, h01)

        def rows_products(b, adv_name, g_name):
            cols = slice(P * (b % 2), P * (b % 2 + 1))
            h = (h_q[1][0][:, cols], h_q[1][1][:, cols])
            adv = psum.tile([P, 4, Z], F32, name=adv_name)
            for u in range(2):
                product(adv[:, 2 * u : 2 * u + 2].rearrange("p a z -> p (a z)"), h, (wa_q[u][0][:], wa_q[u][1][:]))
            g = psum.tile([P, Z], F32, name=g_name)
            for a in range(4):
                product(g[:], h, action(a), a == 0, False)
            product(g[:], h, value, False, True)
            return adv, g

        def rows_max(b, adv):
            mx = sb(f"mx{b}", [P, Z], F32)
            nc.vector.tensor_reduce(mx[:], adv[:].rearrange("p a z -> p z a"), AX.X, ALU.max)
            return mx

        def rows_logits(b, mx, g):
            y = sb(f"y{b}", [P, Z], F32)
            nc.vector.scalar_tensor_tensor(y[:], g[:], -0.25, mx[:], ALU.mult, ALU.add)
            return y

        adv2, g2 = rows_products(2, "adv2", "h_bank1")
        adv3, g3 = rows_products(3, "h_bank0", "h_bank2")

        c23 = sb("c23", [P, 2, 256], F32)
        nc.scalar.activation(c23[:], hi[:], ACT.Copy, scale=-0.25)
        c01 = sb("c01", [P, 2, 256], F32)
        nc.scalar.activation(c01[:], lo[:], ACT.Copy, scale=-0.25)
        pair = sb("pair", [P, 2, 256], F32)
        nc.vector.scalar_tensor_tensor(pair[:], c23[:], -4.0, lo[:], ALU.mult, ALU.max)
        cv = sb("cv", [P, 256], F32)
        nc.scalar.activation(cv[:], vv[:], ACT.Copy, scale=-0.25)
        best = sb("best", [P, 256], F32)
        nc.vector.tensor_tensor(best[:], pair[:, 0], pair[:, 1], ALU.max)
        mx2 = rows_max(2, adv2)
        y2 = rows_logits(2, mx2, g2)
        mx3 = rows_max(3, adv3)
        ys = [psum.tile([P, Z], F32, name=name) for name in ("h_bank3", "hi")]
        terms = [c23[:, 0], c23[:, 1], c01[:, 0], c01[:, 1], cv[:], best[:]]
        for n, term in enumerate(terms):
            for i in range(2):
                nc.tensor.matmul(ys[i][:], lhsT=term[:, P * i : P * (i + 1)], rhs=ident[:], is_transpose=True, start=n == 0, stop=n == len(terms) - 1)
        y3 = rows_logits(3, mx3, g3)
        softmax(2, y2[:])
        softmax(0, ys[0][:])
        softmax(1, ys[1][:])
        softmax(3, y3[:])
